import numpy as np
CORES = [96,97,98,99,224,225,226,227,352,353,354,355,480,481,482,483]
N = 16
ROOT = 10
WIDTHS = [12,12,0,64,64,128,12,12,64,64,0,12,12,128,0,0]
OFF = [0,12,24,24,88,152,280,292,304,368,432,432,444,456,584,584]
C = 584
def setup_inputs(rng):
    return {"x": rng.standard_normal((N, 128, C), dtype=np.float32)}
def reference(x):
    YW = max(WIDTHS)
    y = np.full((N, 128, YW), np.nan, x.dtype)
    for r in range(N):
        y[r][:, :WIDTHS[r]] = x[ROOT][:, OFF[r]:OFF[r] + WIDTHS[r]]
    return {"y": y}

@@ -1,0 +1,77 @@
+SCRATCH = {
+    "buf": ("sbuf", [128, 584], "float32"),
+}
+SEMAPHORES = ["ld_far", "ld_cable", "ld_near", "arrived", "sent", "stored"]
+
+
+def _engines(mask):
+    return bin(mask).count("1")
+
+
+def _plan(T, topo):
+    widths = T.tables["WIDTHS"]
+    root = T.cores[T.root]
+    direct, far = [], []
+    for r, c in enumerate(T.cores):
+        if widths[r] == 0 or c == root:
+            continue
+        if topo.may_write(root, c):
+            direct.append(r)
+        else:
+            far.append(r)
+    relay = None
+    for r, c in enumerate(T.cores):
+        if (relay is None and widths[r] == 0 and c != root and topo.same_plane(root, c)
+                and all(topo.may_write(c, T.cores[f]) for f in far)):
+            relay = c
+    return direct, far, relay
+
+
+def rank_program(g, core, T, topo):
+    rank = T.rank_of(core)
+    if rank is None:
+        return
+    widths, off = T.tables["WIDTHS"], T.tables["OFF"]
+    root = T.cores[T.root]
+    direct, far, relay = _plan(T, topo)
+    far_lo = min(off[r] for r in far)
+    far_hi = max(off[r] + widths[r] for r in far)
+
+    def send(dst, lo, hi, dst_lo):
+        rid, pid = topo.addr(dst, core)
+        m = topo.mask(core, dst)
+        g.remote_dma(T.buf[:, dst_lo:dst_lo + hi - lo], T.buf[:, lo:hi], T.sem.arrived, T.sem.sent, pid, rid, m)
+        return _engines(m)
+
+    if core == root:
+        cable = [r for r in direct if topo.rack(topo.host(T.cores[r])) != topo.rack(topo.host(root))]
+        near = [r for r in direct if r not in cable]
+        blocks = [(far, T.sem.ld_far, g.sync), (cable, T.sem.ld_cable, g.scalar), (near, T.sem.ld_near, g.sync)]
+        for rs, sem, q in blocks:
+            lo, hi = min(off[r] for r in rs), max(off[r] + widths[r] for r in rs)
+            q.dma_start(T.buf[:, lo:hi], T.x[:, lo:hi]).then_inc(sem, 16)
+        n = 0
+        g.wait_ge(T.sem.ld_far, 16)
+        n += send(relay, far_lo, far_hi, 0)
+        for rs, sem in ((cable, T.sem.ld_cable), (near, T.sem.ld_near)):
+            g.wait_ge(sem, 16)
+            for r in sorted(rs, key=lambda r: (topo.host(T.cores[r]) == topo.host(root), -widths[r])):
+                n += send(T.cores[r], off[r], off[r] + widths[r], 0)
+        g.wait_ge(T.sem.sent, n)
+        return
+
+    if core == relay:
+        g.wait_ge(T.sem.arrived, _engines(topo.mask(root, core)))
+        n = 0
+        for r in sorted(far, key=lambda r: -widths[r]):
+            n += send(T.cores[r], off[r] - far_lo, off[r] - far_lo + widths[r], 0)
+        g.wait_ge(T.sem.sent, n)
+        return
+
+    w = widths[rank]
+    if w == 0:
+        return
+    sender = relay if rank in far else root
+    g.sync.wait_ge(T.sem.arrived, _engines(topo.mask(sender, core)))
+    g.sync.dma_start(T.y[:, 0:w], T.buf[:, 0:w]).then_inc(T.sem.stored, 16)
+    g.sync.wait_ge(T.sem.stored, 16)

@@ -1,7 +1,9 @@
 SCRATCH = {
-    "buf": ("sbuf", [128, 584], "float32"),
+    "p12": ("dram", [6, 128, 12], "float32"),
+    "p64": ("dram", [4, 128, 64], "float32"),
+    "p128": ("dram", [2, 128, 128], "float32"),
 }
-SEMAPHORES = ["ld_far", "ld_cable", "ld_near", "arrived", "sent", "stored"]
+SEMAPHORES = ["ld%d" % k for k in range(12)] + ["arr0", "arr1", "sent", "stored"]
 
 
 def _engines(mask):
@@ -11,20 +13,26 @@ def _engines(mask):
 def _plan(T, topo):
     widths = T.tables["WIDTHS"]
     root = T.cores[T.root]
-    direct, far = [], []
-    for r, c in enumerate(T.cores):
-        if widths[r] == 0 or c == root:
-            continue
-        if topo.may_write(root, c):
-            direct.append(r)
-        else:
-            far.append(r)
-    relay = None
-    for r, c in enumerate(T.cores):
-        if (relay is None and widths[r] == 0 and c != root and topo.same_plane(root, c)
-                and all(topo.may_write(c, T.cores[f]) for f in far)):
-            relay = c
-    return direct, far, relay
+    owners = [r for r in range(len(T.cores)) if widths[r] > 0 and T.cores[r] != root]
+    far = [r for r in owners if not topo.may_write(root, T.cores[r])]
+    relays = [c for r, c in enumerate(T.cores)
+              if widths[r] == 0 and topo.same_plane(root, c) and all(topo.may_write(c, T.cores[f]) for f in far)]
+    load = {c: [] for c in relays}
+    for r in sorted(far, key=lambda r: -widths[r]):
+        c = min(relays, key=lambda c: sum(widths[q] for q in load[c]))
+        load[c].append(r)
+    stop = {r: c for c in relays for r in load[c]}
+
+    def way(r):
+        c = T.cores[r]
+        if r in far:
+            return 0
+        if topo.rack(topo.host(c)) != topo.rack(topo.host(root)):
+            return 1
+        return 2 if topo.host(c) != topo.host(root) else 3
+
+    order = sorted(owners, key=lambda r: (way(r), -widths[r], r))
+    return [(r, stop.get(r, T.cores[r])) for r in order], load
 
 
 def rank_program(g, core, T, topo):
@@ -33,45 +41,43 @@ def rank_program(g, core, T, topo):
         return
     widths, off = T.tables["WIDTHS"], T.tables["OFF"]
     root = T.cores[T.root]
-    direct, far, relay = _plan(T, topo)
-    far_lo = min(off[r] for r in far)
-    far_hi = max(off[r] + widths[r] for r in far)
+    order, load = _plan(T, topo)
 
-    def send(dst, lo, hi, dst_lo):
+    def slot(r):
+        w = widths[r]
+        return T["p%d" % w][sum(1 for q in range(r) if widths[q] == w)]
+
+    def send(r, dst, k):
         rid, pid = topo.addr(dst, core)
         m = topo.mask(core, dst)
-        g.remote_dma(T.buf[:, dst_lo:dst_lo + hi - lo], T.buf[:, lo:hi], T.sem.arrived, T.sem.sent, pid, rid, m)
+        g.remote_dma(slot(r), slot(r), T.sem["arr%d" % k], T.sem.sent, pid, rid, m)
         return _engines(m)
 
     if core == root:
-        cable = [r for r in direct if topo.rack(topo.host(T.cores[r])) != topo.rack(topo.host(root))]
-        near = [r for r in direct if r not in cable]
-        blocks = [(far, T.sem.ld_far, g.sync), (cable, T.sem.ld_cable, g.scalar), (near, T.sem.ld_near, g.sync)]
-        for rs, sem, q in blocks:
-            lo, hi = min(off[r] for r in rs), max(off[r] + widths[r] for r in rs)
-            q.dma_start(T.buf[:, lo:hi], T.x[:, lo:hi]).then_inc(sem, 16)
+        for k, (r, _) in enumerate(order):
+            q = g.sync if k % 2 == 0 else g.scalar
+            q.dma_start(slot(r), T.x[:, off[r]:off[r] + widths[r]]).then_inc(T.sem["ld%d" % k], 16)
         n = 0
-        g.wait_ge(T.sem.ld_far, 16)
-        n += send(relay, far_lo, far_hi, 0)
-        for rs, sem in ((cable, T.sem.ld_cable), (near, T.sem.ld_near)):
-            g.wait_ge(sem, 16)
-            for r in sorted(rs, key=lambda r: (topo.host(T.cores[r]) == topo.host(root), -widths[r])):
-                n += send(T.cores[r], off[r], off[r] + widths[r], 0)
+        for k, (r, dst) in enumerate(order):
+            g.wait_ge(T.sem["ld%d" % k], 16)
+            n += send(r, dst, load[dst].index(r) if dst in load else 0)
         g.wait_ge(T.sem.sent, n)
         return
 
-    if core == relay:
-        g.wait_ge(T.sem.arrived, _engines(topo.mask(root, core)))
+    if core in load:
         n = 0
-        for r in sorted(far, key=lambda r: -widths[r]):
-            n += send(T.cores[r], off[r] - far_lo, off[r] - far_lo + widths[r], 0)
+        for k, r in enumerate(load[core]):
+            g.wait_ge(T.sem["arr%d" % k], _engines(topo.mask(root, core)))
+            n += send(r, T.cores[r], 0)
         g.wait_ge(T.sem.sent, n)
         return
 
     w = widths[rank]
     if w == 0:
         return
-    sender = relay if rank in far else root
-    g.sync.wait_ge(T.sem.arrived, _engines(topo.mask(sender, core)))
-    g.sync.dma_start(T.y[:, 0:w], T.buf[:, 0:w]).then_inc(T.sem.stored, 16)
+    sender = dict(order)[rank]
+    if sender == core:
+        sender = root
+    g.sync.wait_ge(T.sem.arr0, _engines(topo.mask(sender, core)))
+    g.sync.dma_start(T.y[:, 0:w], slot(rank)).then_inc(T.sem.stored, 16)
     g.sync.wait_ge(T.sem.stored, 16)

SCRATCH = {
    "p12": ("dram", [6, 128, 12], "float32"),
    "p64": ("dram", [4, 128, 64], "float32"),
    "p128": ("dram", [2, 128, 128], "float32"),
}
SEMAPHORES = ["ld%d" % k for k in range(12)] + ["arr0", "arr1", "sent", "stored"]


def _engines(mask):
    return bin(mask).count("1")


def _plan(T, topo):
    widths = T.tables["WIDTHS"]
    root = T.cores[T.root]
    owners = [r for r in range(len(T.cores)) if widths[r] > 0 and T.cores[r] != root]
    far = [r for r in owners if not topo.may_write(root, T.cores[r])]
    relays = [c for r, c in enumerate(T.cores)
              if widths[r] == 0 and topo.same_plane(root, c) and all(topo.may_write(c, T.cores[f]) for f in far)]
    load = {c: [] for c in relays}
    for r in sorted(far, key=lambda r: -widths[r]):
        c = min(relays, key=lambda c: sum(widths[q] for q in load[c]))
        load[c].append(r)
    stop = {r: c for c in relays for r in load[c]}

    def way(r):
        c = T.cores[r]
        if r in far:
            return 0
        if topo.rack(topo.host(c)) != topo.rack(topo.host(root)):
            return 1
        return 2 if topo.host(c) != topo.host(root) else 3

    order = sorted(owners, key=lambda r: (way(r), -widths[r], r))
    return [(r, stop.get(r, T.cores[r])) for r in order], load


def rank_program(g, core, T, topo):
    rank = T.rank_of(core)
    if rank is None:
        return
    widths, off = T.tables["WIDTHS"], T.tables["OFF"]
    root = T.cores[T.root]
    order, load = _plan(T, topo)

    def slot(r):
        w = widths[r]
        return T["p%d" % w][sum(1 for q in range(r) if widths[q] == w)]

    def send(r, dst, k):
        rid, pid = topo.addr(dst, core)
        m = topo.mask(core, dst)
        g.remote_dma(slot(r), slot(r), T.sem["arr%d" % k], T.sem.sent, pid, rid, m)
        return _engines(m)

    if core == root:
        for k, (r, _) in enumerate(order):
            q = g.sync if k % 2 == 0 else g.scalar
            q.dma_start(slot(r), T.x[:, off[r]:off[r] + widths[r]]).then_inc(T.sem["ld%d" % k], 16)
        n = 0
        for k, (r, dst) in enumerate(order):
            g.wait_ge(T.sem["ld%d" % k], 16)
            n += send(r, dst, load[dst].index(r) if dst in load else 0)
        g.wait_ge(T.sem.sent, n)
        return

    if core in load:
        n = 0
        for k, r in enumerate(load[core]):
            g.wait_ge(T.sem["arr%d" % k], _engines(topo.mask(root, core)))
            n += send(r, T.cores[r], 0)
        g.wait_ge(T.sem.sent, n)
        return

    w = widths[rank]
    if w == 0:
        return
    sender = dict(order)[rank]
    if sender == core:
        sender = root
    g.sync.wait_ge(T.sem.arr0, _engines(topo.mask(sender, core)))
    g.sync.dma_start(T.y[:, 0:w], slot(rank)).then_inc(T.sem.stored, 16)
    g.sync.wait_ge(T.sem.stored, 16)
